import numpy as np
import ml_dtypes


def mxq(x, axis, fmt="e4m3"):
    dtype, down = {"e4m3": (ml_dtypes.float8_e4m3fn, 7), "e5m2": (ml_dtypes.float8_e5m2, 14)}[fmt]
    v = np.moveaxis(np.asarray(x, np.float32).astype(ml_dtypes.bfloat16).astype(np.float64), axis, -1)
    blocks = v.reshape(v.shape[:-1] + (-1, 32))
    amax = np.abs(blocks).max(-1, keepdims=True)
    byte = np.maximum(np.where(amax > 0, np.frexp(amax)[1] - 1 + 127, 0) - down, 1)
    scale = np.exp2(byte - 127.0)
    codes = (blocks / scale).astype(np.float32).astype(dtype).astype(np.float64)
    return np.moveaxis((codes * scale).reshape(v.shape), -1, axis)


WIDE = False


def mx_kscale(k):
    if not WIDE:
        return np.ones(k)
    levels = np.array([10, -10, 5, -5, 0])
    if k % 512:
        return np.exp2(np.random.permutation(np.resize(levels, k // 32))).repeat(32)
    a = np.empty((k // 512, 16))
    for p in range(k // 512):
        a[p, :8] = np.random.permutation(np.resize(levels, 8))
        for g in range(8):
            far = levels[np.abs(levels - a[p, g]) >= 10]
            a[p, g + 8] = far[np.random.randint(len(far))]
    return np.exp2(a.ravel()).repeat(32)


def f64(x):
    return np.asarray(x).astype(np.float64)


def striped(idx):
    return np.tile(idx.reshape(-1, 16).T, (8, 1)).astype(np.uint16)


def unstriped(offs):
    return offs[:16].T.reshape(-1).astype(np.int64)


E2M1 = np.array([0.0, 0.5, 1.0, 1.5, 2.0, 3.0, 4.0, 6.0, -0.0, -0.5, -1.0, -1.5, -2.0, -3.0, -4.0, -6.0])


def pack_weight(w, fmt):
    k, n = w.shape
    w = f64(np.asarray(w, np.float32).astype(ml_dtypes.bfloat16)).reshape(k // 32, 32, n)
    amax = np.abs(w).max(1)
    if fmt == "e4m3":
        byte = np.frexp(amax)[1] - 1 + 127 - 7
    else:
        mant, ex = np.frexp(amax / 6.0)
        byte = np.where(mant > 0.5, ex, ex - 1) + 127
    byte = np.clip(np.where(amax > 0, byte, 1), 1, 254)
    scaled = (w * np.exp2(127.0 - byte)[:, None, :]).reshape(k, n).astype(np.float32)
    by_word = np.ascontiguousarray(scaled.reshape(k // 512, 128, 4, n).transpose(0, 1, 3, 2))
    if fmt == "e4m3":
        words = by_word.astype(ml_dtypes.float8_e4m3fn).view(np.uint8)
    else:
        c = by_word.astype(ml_dtypes.float4_e2m1fn).view(np.uint8) & 0xF
        words = (c[..., 0::2] | (c[..., 1::2] << 4)).reshape(k // 512, 128, 2 * n)
    return np.ascontiguousarray(words), np.ascontiguousarray(byte.astype(np.uint8).reshape(k // 512, 16, n))


def unpack_weight(words, scales, fmt):
    g, _, n = scales.shape
    words = np.ascontiguousarray(words).reshape(g, 128, n, -1)
    if fmt == "e4m3":
        vals = words.view(ml_dtypes.float8_e4m3fn).astype(np.float64)
    else:
        nib = np.empty((g, 128, n, 4), np.uint8)
        nib[..., 0::2] = words & 0xF
        nib[..., 1::2] = words >> 4
        vals = E2M1[nib]
    vals = vals * np.repeat(np.exp2(scales.astype(np.float64) - 127.0), 8, axis=1)[..., None]
    return vals.transpose(0, 1, 3, 2).reshape(g * 512, n)


def gelu(v):
    return 0.5 * v * (1.0 + np.tanh(np.sqrt(2.0 / np.pi) * (v + 0.044715 * v**3)))


def bf(x):
    return np.asarray(x, np.float32).astype(ml_dtypes.bfloat16)


def planes(Y):
    n, m = Y.shape
    b = f64(bf(Y)).reshape(n // 32, 32, m)
    amax = np.abs(b).max(1)
    byte = np.clip(np.where(amax > 0, np.frexp(amax)[1] - 1 + 127 - 7, 1), 1, 254)
    codes = (b * np.exp2(127.0 - byte)[:, None, :]).reshape(n, m).astype(np.float32).astype(ml_dtypes.float8_e4m3fn).view(np.uint8)
    words = codes.reshape(n // 512, 128, 4, m).transpose(0, 1, 3, 2)
    return np.ascontiguousarray(words), np.ascontiguousarray(byte.astype(np.uint8).reshape(n // 512, 16, m))


K, T, S, P, H, N = 1024, 2048, 1024, 512, 512, 1024

def setup_inputs():
    n = np.random.standard_normal
    s = mx_kscale(K)[:, None]
    u = mx_kscale(H)[:, None]
    tab_words, tab_scales = pack_weight(n((K, T)) * s, "e4m3")
    w2_words, w2_scales = pack_weight(n((K, H)) / s / np.sqrt(K), "e2m1")
    wb_words, wb_scales = pack_weight(0.6 * n((H, N)) / u / np.sqrt(H), "e4m3")
    return {
        "tab_words": tab_words, "tab_scales": tab_scales,
        "offs": striped(np.random.permutation(T)[:S]),
        "pos1": striped(np.random.permutation(S)[:P]),
        "pos2": striped(np.random.permutation(S)[:P]),
        "w1": (n((K, H)) / s * u.T / np.sqrt(K)).astype(np.float32),
        "b1": (0.5 * n(H) * u[:, 0]).astype(np.float32),
        "w2_words": w2_words, "w2_scales": w2_scales,
        "gain": (np.random.uniform(0.5, 1.5, H) * u[:, 0]).astype(np.float32),
        "wa": (0.6 * n((H, N)) / u / np.sqrt(H)).astype(np.float32),
        "wb_words": wb_words, "wb_scales": wb_scales,
        "limit": n(N).astype(np.float32),
        "base": np.random.uniform(0.1, 0.9, N).astype(np.float32),
        "gy": (3.0 * np.exp(0.8 * n(N))).astype(np.float32),
    }

def reference(tab_words, tab_scales, offs, pos1, pos2, w1, b1, w2_words, w2_scales, gain, wa, wb_words, wb_scales, limit, base, gy):
    v = unpack_weight(tab_words, tab_scales, "e4m3")[:, unstriped(offs)]
    w2 = unpack_weight(w2_words, w2_scales, "e2m1")
    wb = unpack_weight(wb_words, wb_scales, "e4m3")
    h = (mxq(f64(w1), 0, "e4m3").T @ v) + f64(b1)[:, None]
    f = np.abs(w2.T @ v) * f64(gain)[:, None]
    e = mxq(f64(wa), 0, "e4m3").T @ mxq(h, 0, "e4m3") + wb.T @ mxq(f, 0, "e4m3")
    a = 1.0 / (1.0 + np.exp(-(e[:, unstriped(pos1)] + f64(limit)[:, None])))
    c = e[:, unstriped(pos2)]
    y = (a - f64(base)[:, None]) * c * f64(gy)[:, None]
    words, scales = planes(y)
    return y, words, scales

@@ -1,0 +1,319 @@
+from contextlib import ExitStack
+
+import concourse.mybir as mybir
+
+K, T, S, PICKS, H, N = 1024, 2048, 1024, 512, 512, 1024
+FLOPS = 2 * (2 * K * H * S + 2 * H * N * S)
+
+F32 = mybir.dt.float32
+BF16 = mybir.dt.bfloat16
+I32 = mybir.dt.int32
+U32 = mybir.dt.uint32
+U16 = mybir.dt.uint16
+U8 = mybir.dt.uint8
+E4M3X4 = mybir.dt.float8_e4m3fn_x4
+E2M1X4 = mybir.dt.float4_e2m1fn_x4
+ALU = mybir.AluOpType
+ACT = mybir.ActivationFunctionType
+
+P = 128
+PACK = 4
+K_PASS = P * PACK
+PASSES = K // K_PASS
+GROUPS = N // K_PASS
+HALF = S // 2
+BLOCK = 128
+QUADS = 4
+
+
+def tile_list_beam_hop_scores_kernel(
+    tc, tab_words, tab_scales, offs, pos1, pos2, w1, b1, w2_words, w2_scales, gain, wa, wb_words, wb_scales,
+    limit, base, gy, out_0, out_1, out_2,
+):
+    nc = tc.nc
+    with ExitStack() as ctx:
+        held = ctx.enter_context(tc.tile_pool(name="held", bufs=1))
+        ring = ctx.enter_context(tc.tile_pool(name="ring", bufs=3))
+        psum = ctx.enter_context(tc.psum_pool(name="psum", bufs=8))
+
+        def keep(name, shape, dtype):
+            return held.tile(shape, dtype, name=name, align_bytes=64)
+
+        offs_t = held.tile([P, S // 16], U16, name="offs_t")
+        pos1_t = held.tile([P, PICKS // 16], U16, name="pos1_t")
+        pos2_t = held.tile([P, PICKS // 16], U16, name="pos2_t")
+
+        tab_scale_rows = keep("tab_scale_rows", [P, T // 4], I32)
+        weight_scale_rows = keep("weight_scale_rows", [P, N // 4], I32)
+        v_scales_second = keep("v_scales_second", [P, S // 4], I32)
+        nc.gpsimd.memset(tab_scale_rows[:], 0)
+        nc.vector.memset(weight_scale_rows[:], 0)
+        nc.vector.memset(v_scales_second[:], 0)
+
+        w1_raw = [keep(f"w1_raw{a}", [P, PACK, H], F32) for a in range(PASSES)]
+        wa_raw = [keep(f"wa_raw{g}", [P, PACK, K_PASS], F32) for g in range(GROUPS)]
+        tab = [keep(f"tab{a}", [P, T], I32) for a in range(PASSES)]
+        w2_raw = keep("w2_raw", [P, PASSES, H // 2], I32)
+        wb_raw = keep("wb_raw", [P, N], I32)
+        b1_t = keep("b1_t", [P, PACK], F32)
+        gain_t = keep("gain_t", [P, PACK], F32)
+        limit_t = keep("limit_t", [P, GROUPS, PACK], F32)
+        base_t = keep("base_t", [P, GROUPS, PACK], F32)
+        gy_t = keep("gy_t", [P, GROUPS, PACK], F32)
+
+        def load_w1(a):
+            nc.sync.dma_start(out=w1_raw[a][:], in_=w1[a * K_PASS : (a + 1) * K_PASS, :].rearrange("(p j) c -> p j c", j=PACK))
+
+        def load_tab(a):
+            nc.sync.dma_start(out=tab[a][:], in_=tab_words[a].rearrange("p t i -> p (t i)").bitcast(I32))
+
+        def load_wa(g):
+            nc.sync.dma_start(
+                out=wa_raw[g][:], in_=wa[:, g * K_PASS : (g + 1) * K_PASS].rearrange("(p j) c -> p j c", j=PACK)
+            )
+
+        def load_w2_scales(q):
+            nc.sync.dma_start(
+                out=weight_scale_rows[32 * q : 32 * q + 4, :].rearrange("r (a c) -> r a c", a=PASSES),
+                in_=w2_scales[:, 4 * q : 4 * q + 4, :].bitcast(I32).rearrange("a r c -> r a c"),
+            )
+
+        nc.sync.dma_start(offs_t[:], offs)
+        for q in range(QUADS):
+            nc.sync.dma_start(
+                out=tab_scale_rows[32 * q : 32 * q + 8, :], in_=tab_scales[:, 4 * q : 4 * q + 4, :].bitcast(I32)
+            )
+        load_w2_scales(0)
+        load_w2_scales(1)
+        load_tab(0)
+        load_w2_scales(2)
+        load_w2_scales(3)
+        for q in range(QUADS):
+            nc.sync.dma_start(
+                out=weight_scale_rows[32 * q + 4 : 32 * q + 8, :], in_=wb_scales[0, 4 * q : 4 * q + 4, :].bitcast(I32)
+            )
+        load_tab(1)
+        nc.sync.dma_start(out=w2_raw[:], in_=w2_words.bitcast(I32).rearrange("a p c -> p a c"))
+        v_scales = keep("v_scales", [P, S // 4], I32)
+        nc.vector.tensor_copy(out=v_scales[:].bitcast(U8), in_=tab_scale_rows[:].bitcast(U8).indirect(offs_t[:]))
+        for q in range(QUADS):
+            nc.sync.dma_start(out=v_scales_second[32 * q : 32 * q + 4, :], in_=v_scales[32 * q + 4 : 32 * q + 8, :])
+        load_w1(0)
+        nc.sync.dma_start(out=gain_t[:], in_=gain.rearrange("(p t) -> p t", t=PACK))
+        load_w1(1)
+        nc.sync.dma_start(out=b1_t[:], in_=b1.rearrange("(p t) -> p t", t=PACK))
+        load_wa(0)
+        nc.sync.dma_start(out=wb_raw[:], in_=wb_words[0].rearrange("p c i -> p (c i)").bitcast(I32))
+        nc.sync.dma_start(pos1_t[:], pos1)
+        nc.sync.dma_start(pos2_t[:], pos2)
+        load_wa(1)
+        for vec_t, vec in ((limit_t, limit), (base_t, base), (gy_t, gy)):
+            nc.sync.dma_start(out=vec_t[:], in_=vec.rearrange("(g p t) -> p g t", g=GROUPS, t=PACK))
+
+        def round_and_deal(name, raw, copy, pieces):
+            rounded = keep(name, [P, PACK * K_PASS], BF16)
+            for piece in range(pieces):
+                ms = slice(piece * P // pieces, (piece + 1) * P // pieces)
+                copy(
+                    out=rounded[:].rearrange("p (t m j) -> p m j t", t=PACK, j=PACK)[:, ms],
+                    in_=raw[:].rearrange("p j (m t) -> p m j t", t=PACK)[:, ms],
+                )
+            return rounded
+
+        def quantize(codes, scales, rounded):
+            nc.vector.quantize_mx(out=codes.bitcast(E4M3X4), scales=scales, in_=rounded)
+
+        v_planes = [v_scales[:].bitcast(U8), v_scales_second[:].bitcast(U8)]
+
+        weight_scales = keep("weight_scales", [P, N], U8)
+        nc.vector.tensor_copy(
+            out=weight_scales[:].rearrange("p (a t m) -> p a m t", a=2, t=PACK),
+            in_=weight_scale_rows[:].bitcast(U8).rearrange("p (a m t) -> p a m t", a=2, t=PACK),
+        )
+        w2_codes = keep("w2_codes", [P, PASSES * H], U16)
+        nc.scalar.copy(
+            out=w2_codes[:].rearrange("p (a t m) -> p a m t", a=PASSES, t=PACK),
+            in_=w2_raw[:].rearrange("p a c -> p (a c)").bitcast(U16).rearrange("p (a m t) -> p a m t", a=PASSES, t=PACK),
+        )
+
+        v_codes = [[keep(f"v_codes{a}_{half}", [P, HALF], U32) for half in range(2)] for a in range(PASSES)]
+
+        def gather_words(a, half):
+            cols = slice(half * HALF // 16, (half + 1) * HALF // 16)
+            nc.vector.tensor_copy(out=v_codes[a][half][:], in_=tab[a][:].bitcast(U32).indirect(offs_t[:, cols]))
+
+        w1_codes = keep("w1_codes", [P, PASSES, H], U32)
+        w1_scales = keep("w1_scales", [P, PASSES, H], U8)
+        gather_words(0, 0)
+        gather_words(0, 1)
+        gather_words(1, 0)
+        gather_words(1, 1)
+
+        def first_stage(half, block, lhs):
+            bank = psum.tile([P, PACK, BLOCK], F32, name="bank")
+            cols = slice(block * BLOCK, (block + 1) * BLOCK)
+            plane_cols = slice(half * HALF + block * BLOCK, half * HALF + (block + 1) * BLOCK)
+            for t in range(PACK):
+                for a in range(PASSES):
+                    codes, scales = lhs(a, t)
+                    nc.tensor.matmul_mx(
+                        out=bank[:, t, :], lhsT=codes, lhsT_scale=scales,
+                        rhs=v_codes[a][half][:, cols].bitcast(E4M3X4), rhs_scale=v_planes[a][:, plane_cols],
+                        start=(a == 0), stop=(a == PASSES - 1),
+                    )
+            return bank
+
+        def w2_slice(a, t):
+            cols = slice(a * H + t * P, a * H + (t + 1) * P)
+            return w2_codes[:, cols].bitcast(U8).bitcast(E2M1X4), weight_scales[:, cols]
+
+        def w1_slice(a, t):
+            cols = slice(t * P, (t + 1) * P)
+            return w1_codes[:, a, cols].bitcast(E4M3X4), w1_scales[:, a, cols]
+
+        blocks = HALF // BLOCK
+        f_codes = keep("f_codes", [P, S], U32)
+        f_scales = keep("f_scales", [P, S], U8)
+        h_codes = keep("h_codes", [P, S], U32)
+        h_scales = keep("h_scales", [P, S], U8)
+        f_rounded = [keep(f"f_rounded{half}", [P, HALF, PACK], BF16) for half in range(2)]
+        h_rounded = [keep(f"h_rounded{half}", [P, HALF, PACK], BF16) for half in range(2)]
+
+        def deviation(half, pair):
+            size = keep(f"size{half}_{pair}", [P, 2 * BLOCK, PACK], F32)
+            for b in range(2):
+                bank = first_stage(half, 2 * pair + b, w2_slice)
+                nc.scalar.activation(
+                    out=size[:, b * BLOCK : (b + 1) * BLOCK, :], in_=bank[:].rearrange("p t n -> p n t"), func=ACT.Abs
+                )
+            return size
+
+        def apply_gain(half, pair, size):
+            nc.vector.tensor_tensor(
+                out=f_rounded[half][:, 2 * pair * BLOCK : 2 * (pair + 1) * BLOCK, :], in0=size[:],
+                in1=gain_t[:].unsqueeze(1).to_broadcast([P, 2 * BLOCK, PACK]), op=ALU.mult,
+            )
+
+        def h_half(half):
+            for block in range(blocks):
+                bank = first_stage(half, block, w1_slice)
+                nc.vector.tensor_tensor(
+                    out=h_rounded[half][:, block * BLOCK : (block + 1) * BLOCK, :], in0=bank[:].rearrange("p t n -> p n t"),
+                    in1=b1_t[:].unsqueeze(1).to_broadcast([P, BLOCK, PACK]), op=ALU.add,
+                )
+
+        def quantize_half(codes, scales, rounded, half):
+            cols = slice(half * HALF, (half + 1) * HALF)
+            quantize(codes[:, cols], scales[:, cols], rounded[half][:].rearrange("p n t -> p (n t)"))
+
+        sizes = [[deviation(half, pair) for pair in range(2)] for half in range(2)]
+        w1_first = round_and_deal("w1_rounded0", w1_raw[0], nc.vector.tensor_copy, 1)
+        apply_gain(0, 0, sizes[0][0])
+        quantize(w1_codes[:, 0, :], w1_scales[:, 0, :], w1_first[:])
+        w1_second = round_and_deal("w1_rounded1", w1_raw[1], nc.vector.tensor_copy, 1)
+        apply_gain(0, 1, sizes[0][1])
+        quantize(w1_codes[:, 1, :], w1_scales[:, 1, :], w1_second[:])
+
+        wa_first = round_and_deal("wa_rounded0", wa_raw[0], nc.scalar.copy, 4)
+        wb_codes = keep("wb_codes", [P, N], U32)
+        nc.scalar.copy(
+            out=wb_codes[:].rearrange("p (g t m) -> p g m t", g=GROUPS, t=PACK),
+            in_=wb_raw[:].bitcast(U32).rearrange("p (g m t) -> p g m t", g=GROUPS, t=PACK),
+        )
+        wa_codes = keep("wa_codes", [P, GROUPS, K_PASS], U32)
+        wa_scales = keep("wa_scales", [P, GROUPS, K_PASS], U8)
+
+        e_tiles = [[keep(f"e{g}_{t}", [P, S], F32) for t in range(PACK)] for g in range(GROUPS)]
+
+        def scores(g, t, half, copy):
+            cols = slice(t * P, (t + 1) * P)
+            n_cols = slice(g * K_PASS + t * P, g * K_PASS + (t + 1) * P)
+            bank = psum.tile([P, HALF], F32, name="bank")
+            tokens = slice(half * HALF, (half + 1) * HALF)
+            nc.tensor.matmul_mx(
+                out=bank[:], lhsT=wb_codes[:, n_cols].bitcast(E4M3X4), lhsT_scale=weight_scales[4:P, n_cols],
+                rhs=f_codes[:, tokens].bitcast(E4M3X4), rhs_scale=f_scales[:, tokens], start=True, stop=False,
+            )
+            nc.tensor.matmul_mx(
+                out=bank[:], lhsT=wa_codes[:, g, cols].bitcast(E4M3X4), lhsT_scale=wa_scales[:, g, cols],
+                rhs=h_codes[:, tokens].bitcast(E4M3X4), rhs_scale=h_scales[:, tokens], start=False, stop=True,
+            )
+            copy(out=e_tiles[g][t][:, tokens], in_=bank[:])
+
+        wa_second = round_and_deal("wa_rounded1", wa_raw[1], nc.scalar.copy, 4)
+        quantize_half(f_codes, f_scales, f_rounded, 0)
+        h_half(0)
+        quantize(wa_codes[:, 0, :], wa_scales[:, 0, :], wa_first[:])
+        quantize_half(h_codes, h_scales, h_rounded, 0)
+        apply_gain(1, 0, sizes[1][0])
+        apply_gain(1, 1, sizes[1][1])
+        quantize(wa_codes[:, 1, :], wa_scales[:, 1, :], wa_second[:])
+        quantize_half(f_codes, f_scales, f_rounded, 1)
+        h_half(1)
+        for g in range(GROUPS):
+            for t in range(PACK):
+                scores(g, t, 0, nc.scalar.copy)
+        quantize_half(h_codes, h_scales, h_rounded, 1)
+        for t in range(3):
+            scores(0, t, 1, nc.vector.tensor_copy)
+
+        y_codes = keep("y_codes", [P, GROUPS, PICKS], I32)
+        y_scales = keep("y_scales", [P, PICKS // 4], I32)
+        out_rows = out_0.rearrange("(g p t) m -> g p t m", g=GROUPS, t=PACK)
+
+        def look(e, y, g, t, lo, hi):
+            a_val = ring.tile([P, PICKS], F32, name="a_val")
+            weight = ring.tile([P, PICKS], F32, name="weight")
+            width = hi - lo
+            nc.scalar.activation(
+                out=a_val[:, 0:width], in_=e[:].indirect(pos1_t[:, lo // 16 : hi // 16]), func=ACT.Sigmoid,
+                bias=limit_t[:, g, t : t + 1],
+            )
+            nc.vector.tensor_scalar(
+                out=weight[:, 0:width], in0=a_val[:, 0:width], scalar1=base_t[:, g, t : t + 1], scalar2=gy_t[:, g, t : t + 1],
+                op0=ALU.subtract, op1=ALU.mult,
+            )
+            nc.vector.tensor_tensor(
+                out=y[:, t, :], in0=e[:].indirect(pos2_t[:, lo // 16 : hi // 16]), in1=weight[:, 0:width], op=ALU.mult
+            )
+            nc.sync.dma_start(out=out_rows[g, :, t, lo:hi], in_=y[:, t, :])
+
+        def round_y(y, g, lo, hi):
+            rounded = keep(f"y_rounded{g}_{lo}", [P, hi - lo, PACK], BF16)
+            nc.vector.tensor_copy(
+                out=rounded[:].rearrange("p (c i) t -> p c t i", i=4), in_=y[:].rearrange("p t (c i) -> p c t i", i=4)
+            )
+            return rounded
+
+        def planes(rounded, g, lo, hi):
+            quantize(y_codes[:, g, lo:hi], y_scales[4 * g : P, :].bitcast(U8)[:, lo:hi], rounded[:].rearrange("p m t -> p (m t)"))
+            nc.sync.dma_start(
+                out=out_1[g].rearrange("p m i -> p (m i)").bitcast(I32)[:, lo:hi], in_=y_codes[:, g, lo:hi]
+            )
+
+        y_first = keep("y_first", [P, PACK, PICKS], F32)
+        y_low = keep("y_low", [P, PACK, PICKS // 2], F32)
+        y_high = keep("y_high", [P, PACK, PICKS // 2], F32)
+        for t in range(PACK):
+            look(e_tiles[0][t], y_first, 0, t, 0, PICKS)
+            if t == 0:
+                scores(0, PACK - 1, 1, nc.scalar.copy)
+            else:
+                scores(1, t - 1, 1, nc.scalar.copy)
+        scores(1, PACK - 1, 1, nc.scalar.copy)
+        e_last = e_tiles[1]
+        for t in range(PACK):
+            look(e_last[t], y_low, 1, t, 0, PICKS // 2)
+            if t == 0:
+                first_rounded = round_y(y_first, 0, 0, PICKS)
+            if t == 1:
+                planes(first_rounded, 0, 0, PICKS)
+        low_rounded = round_y(y_low, 1, 0, PICKS // 2)
+        for t in range(PACK):
+            look(e_last[t], y_high, 1, t, PICKS // 2, PICKS)
+            if t == 0:
+                planes(low_rounded, 1, 0, PICKS // 2)
+        planes(round_y(y_high, 1, PICKS // 2, PICKS), 1, PICKS // 2, PICKS)
+        for q in range(QUADS):
+            queue = nc.sync if q % 2 == 0 else nc.scalar
+            queue.dma_start(out=out_2[:, 4 * q : 4 * q + 4, :].bitcast(I32), in_=y_scales[32 * q : 32 * q + 8, :])

@@ -36,8 +36,8 @@ def tile_list_beam_hop_scores_kernel(
         ring = ctx.enter_context(tc.tile_pool(name="ring", bufs=3))
         psum = ctx.enter_context(tc.psum_pool(name="psum", bufs=8))
 
-        def keep(name, shape, dtype):
-            return held.tile(shape, dtype, name=name, align_bytes=64)
+        def keep(name, shape, dtype, tag=None):
+            return held.tile(shape, dtype, name=name, tag=tag or name, align_bytes=64)
 
         offs_t = held.tile([P, S // 16], U16, name="offs_t")
         pos1_t = held.tile([P, PICKS // 16], U16, name="pos1_t")
@@ -46,8 +46,8 @@ def tile_list_beam_hop_scores_kernel(
         tab_scale_rows = keep("tab_scale_rows", [P, T // 4], I32)
         weight_scale_rows = keep("weight_scale_rows", [P, N // 4], I32)
         v_scales_second = keep("v_scales_second", [P, S // 4], I32)
-        nc.gpsimd.memset(tab_scale_rows[:], 0)
-        nc.vector.memset(weight_scale_rows[:], 0)
+        nc.vector.memset(tab_scale_rows[:], 0)
+        nc.gpsimd.memset(weight_scale_rows[:], 0)
         nc.vector.memset(v_scales_second[:], 0)
 
         w1_raw = [keep(f"w1_raw{a}", [P, PACK, H], F32) for a in range(PASSES)]
@@ -78,26 +78,29 @@ def tile_list_beam_hop_scores_kernel(
                 in_=w2_scales[:, 4 * q : 4 * q + 4, :].bitcast(I32).rearrange("a r c -> r a c"),
             )
 
-        nc.sync.dma_start(offs_t[:], offs)
-        for q in range(QUADS):
-            nc.sync.dma_start(
-                out=tab_scale_rows[32 * q : 32 * q + 8, :], in_=tab_scales[:, 4 * q : 4 * q + 4, :].bitcast(I32)
-            )
-        load_w2_scales(0)
-        load_w2_scales(1)
-        load_tab(0)
-        load_w2_scales(2)
-        load_w2_scales(3)
-        for q in range(QUADS):
-            nc.sync.dma_start(
+        def load_wb_scales(q, queue):
+            queue.dma_start(
                 out=weight_scale_rows[32 * q + 4 : 32 * q + 8, :], in_=wb_scales[0, 4 * q : 4 * q + 4, :].bitcast(I32)
             )
-        load_tab(1)
+
+        nc.sync.dma_start(offs_t[:], offs)
+        for r in range(4):
+            nc.sync.dma_start(
+                out=tab_scale_rows[r:P:16, :],
+                in_=tab_scales.bitcast(I32).rearrange("a (q r) c -> r q a c", r=4)[r],
+            )
         nc.sync.dma_start(out=w2_raw[:], in_=w2_words.bitcast(I32).rearrange("a p c -> p a c"))
+        load_w2_scales(0)
+        load_tab(0)
+        for q in range(1, QUADS):
+            load_w2_scales(q)
+        for q in range(QUADS):
+            load_wb_scales(q, nc.sync if q < QUADS - 1 else nc.gpsimd)
+        load_tab(1)
         v_scales = keep("v_scales", [P, S // 4], I32)
         nc.vector.tensor_copy(out=v_scales[:].bitcast(U8), in_=tab_scale_rows[:].bitcast(U8).indirect(offs_t[:]))
         for q in range(QUADS):
-            nc.sync.dma_start(out=v_scales_second[32 * q : 32 * q + 4, :], in_=v_scales[32 * q + 4 : 32 * q + 8, :])
+            nc.sync.dma_start(out=v_scales_second[32 * q : 32 * q + 4, :], in_=v_scales[32 * q + 16 : 32 * q + 20, :])
         load_w1(0)
         nc.sync.dma_start(out=gain_t[:], in_=gain.rearrange("(p t) -> p t", t=PACK))
         load_w1(1)
@@ -136,7 +139,10 @@ def tile_list_beam_hop_scores_kernel(
             in_=w2_raw[:].rearrange("p a c -> p (a c)").bitcast(U16).rearrange("p (a m t) -> p a m t", a=PASSES, t=PACK),
         )
 
-        v_codes = [[keep(f"v_codes{a}_{half}", [P, HALF], U32) for half in range(2)] for a in range(PASSES)]
+        v_codes = [
+            [keep("v_codes0_0", [P, HALF], U32), keep("v_codes0_1", [P, HALF], U32, tag="weight_scale_rows")],
+            [keep("v_codes1_0", [P, HALF], U32), keep("v_codes1_1", [P, HALF], U32)],
+        ]
 
         def gather_words(a, half):
             cols = slice(half * HALF // 16, (half + 1) * HALF // 16)
@@ -149,19 +155,21 @@ def tile_list_beam_hop_scores_kernel(
         gather_words(1, 0)
         gather_words(1, 1)
 
-        def first_stage(half, block, lhs):
-            bank = psum.tile([P, PACK, BLOCK], F32, name="bank")
+        def first_stage_pass(bank, half, block, lhs, a):
             cols = slice(block * BLOCK, (block + 1) * BLOCK)
             plane_cols = slice(half * HALF + block * BLOCK, half * HALF + (block + 1) * BLOCK)
             for t in range(PACK):
-                for a in range(PASSES):
-                    codes, scales = lhs(a, t)
-                    nc.tensor.matmul_mx(
-                        out=bank[:, t, :], lhsT=codes, lhsT_scale=scales,
-                        rhs=v_codes[a][half][:, cols].bitcast(E4M3X4), rhs_scale=v_planes[a][:, plane_cols],
-                        start=(a == 0), stop=(a == PASSES - 1),
-                    )
-            return bank
+                codes, scales = lhs(a, t)
+                nc.tensor.matmul_mx(
+                    out=bank[:, t, :], lhsT=codes, lhsT_scale=scales,
+                    rhs=v_codes[a][half][:, cols].bitcast(E4M3X4), rhs_scale=v_planes[a][:, plane_cols],
+                    start=(a == 0 and t == 0), stop=(a == PASSES - 1 and t == PACK - 1),
+                )
+
+        def open_banks(banks, half, lhs):
+            for block in range(HALF // BLOCK):
+                banks[half, block] = psum.tile([P, PACK, BLOCK], F32, name="bank")
+                first_stage_pass(banks[half, block], half, block, lhs, 0)
 
         def w2_slice(a, t):
             cols = slice(a * H + t * P, a * H + (t + 1) * P)
@@ -176,13 +184,13 @@ def tile_list_beam_hop_scores_kernel(
         f_scales = keep("f_scales", [P, S], U8)
         h_codes = keep("h_codes", [P, S], U32)
         h_scales = keep("h_scales", [P, S], U8)
-        f_rounded = [keep(f"f_rounded{half}", [P, HALF, PACK], BF16) for half in range(2)]
         h_rounded = [keep(f"h_rounded{half}", [P, HALF, PACK], BF16) for half in range(2)]
 
         def deviation(half, pair):
             size = keep(f"size{half}_{pair}", [P, 2 * BLOCK, PACK], F32)
             for b in range(2):
-                bank = first_stage(half, 2 * pair + b, w2_slice)
+                bank = f_banks[half, 2 * pair + b]
+                first_stage_pass(bank, half, 2 * pair + b, w2_slice, 1)
                 nc.scalar.activation(
                     out=size[:, b * BLOCK : (b + 1) * BLOCK, :], in_=bank[:].rearrange("p t n -> p n t"), func=ACT.Abs
                 )
@@ -196,7 +204,7 @@ def tile_list_beam_hop_scores_kernel(
 
         def h_half(half):
             for block in range(blocks):
-                bank = first_stage(half, block, w1_slice)
+                bank = h_banks[half, block]
                 nc.vector.tensor_tensor(
                     out=h_rounded[half][:, block * BLOCK : (block + 1) * BLOCK, :], in0=bank[:].rearrange("p t n -> p n t"),
                     in1=b1_t[:].unsqueeze(1).to_broadcast([P, BLOCK, PACK]), op=ALU.add,
@@ -206,20 +214,30 @@ def tile_list_beam_hop_scores_kernel(
             cols = slice(half * HALF, (half + 1) * HALF)
             quantize(codes[:, cols], scales[:, cols], rounded[half][:].rearrange("p n t -> p (n t)"))
 
-        sizes = [[deviation(half, pair) for pair in range(2)] for half in range(2)]
+        f_banks, h_banks = {}, {}
+        open_banks(f_banks, 0, w2_slice)
+        sizes = [[deviation(0, pair) for pair in range(2)]]
         w1_first = round_and_deal("w1_rounded0", w1_raw[0], nc.vector.tensor_copy, 1)
-        apply_gain(0, 0, sizes[0][0])
+        w1_second = round_and_deal("w1_rounded1", w1_raw[1], nc.scalar.copy, 4)
+        f_rounded = [keep("f_rounded0", [P, HALF, PACK], BF16, tag="w1_raw0"), keep("f_rounded1", [P, HALF, PACK], BF16)]
+        open_banks(f_banks, 1, w2_slice)
+        sizes.append([deviation(1, pair) for pair in range(2)])
         quantize(w1_codes[:, 0, :], w1_scales[:, 0, :], w1_first[:])
-        w1_second = round_and_deal("w1_rounded1", w1_raw[1], nc.vector.tensor_copy, 1)
-        apply_gain(0, 1, sizes[0][1])
+        apply_gain(0, 0, sizes[0][0])
         quantize(w1_codes[:, 1, :], w1_scales[:, 1, :], w1_second[:])
+        for half in range(2):
+            open_banks(h_banks, half, w1_slice)
+            for block in range(blocks):
+                first_stage_pass(h_banks[half, block], half, block, w1_slice, 1)
+        apply_gain(0, 1, sizes[0][1])
+        quantize_half(f_codes, f_scales, f_rounded, 0)
 
-        wa_first = round_and_deal("wa_rounded0", wa_raw[0], nc.scalar.copy, 4)
         wb_codes = keep("wb_codes", [P, N], U32)
         nc.scalar.copy(
             out=wb_codes[:].rearrange("p (g t m) -> p g m t", g=GROUPS, t=PACK),
             in_=wb_raw[:].bitcast(U32).rearrange("p (g m t) -> p g m t", g=GROUPS, t=PACK),
         )
+        wa_first = round_and_deal("wa_rounded0", wa_raw[0], nc.scalar.copy, 4)
         wa_codes = keep("wa_codes", [P, GROUPS, K_PASS], U32)
         wa_scales = keep("wa_scales", [P, GROUPS, K_PASS], U8)
 
@@ -240,15 +258,14 @@ def tile_list_beam_hop_scores_kernel(
             )
             copy(out=e_tiles[g][t][:, tokens], in_=bank[:])
 
-        wa_second = round_and_deal("wa_rounded1", wa_raw[1], nc.scalar.copy, 4)
-        quantize_half(f_codes, f_scales, f_rounded, 0)
         h_half(0)
-        quantize(wa_codes[:, 0, :], wa_scales[:, 0, :], wa_first[:])
-        quantize_half(h_codes, h_scales, h_rounded, 0)
         apply_gain(1, 0, sizes[1][0])
         apply_gain(1, 1, sizes[1][1])
-        quantize(wa_codes[:, 1, :], wa_scales[:, 1, :], wa_second[:])
+        quantize(wa_codes[:, 0, :], wa_scales[:, 0, :], wa_first[:])
+        quantize_half(h_codes, h_scales, h_rounded, 0)
         quantize_half(f_codes, f_scales, f_rounded, 1)
+        wa_second = round_and_deal("wa_rounded1", wa_raw[1], nc.scalar.copy, 4)
+        quantize(wa_codes[:, 1, :], wa_scales[:, 1, :], wa_second[:])
         h_half(1)
         for g in range(GROUPS):
             for t in range(PACK):
@@ -256,6 +273,10 @@ def tile_list_beam_hop_scores_kernel(
         quantize_half(h_codes, h_scales, h_rounded, 1)
         for t in range(3):
             scores(0, t, 1, nc.vector.tensor_copy)
+        offset_t = keep("offset_t", [P, PACK], F32)
+        nc.vector.scalar_tensor_tensor(
+            out=offset_t[:], in0=base_t[:, 1, :], scalar=-1.0, in1=gy_t[:, 1, :], op0=ALU.mult, op1=ALU.mult
+        )
 
         y_codes = keep("y_codes", [P, GROUPS, PICKS], I32)
         y_scales = keep("y_scales", [P, PICKS // 4], I32)
@@ -269,20 +290,30 @@ def tile_list_beam_hop_scores_kernel(
                 out=a_val[:, 0:width], in_=e[:].indirect(pos1_t[:, lo // 16 : hi // 16]), func=ACT.Sigmoid,
                 bias=limit_t[:, g, t : t + 1],
             )
-            nc.vector.tensor_scalar(
-                out=weight[:, 0:width], in0=a_val[:, 0:width], scalar1=base_t[:, g, t : t + 1], scalar2=gy_t[:, g, t : t + 1],
-                op0=ALU.subtract, op1=ALU.mult,
-            )
+            if g == 0:
+                nc.vector.tensor_scalar(
+                    out=weight[:, 0:width], in0=a_val[:, 0:width], scalar1=base_t[:, g, t : t + 1],
+                    scalar2=gy_t[:, g, t : t + 1], op0=ALU.subtract, op1=ALU.mult,
+                )
+            else:
+                nc.scalar.activation(
+                    out=weight[:, 0:width], in_=a_val[:, 0:width], func=ACT.Identity,
+                    scale=gy_t[:, g, t : t + 1], bias=offset_t[:, t : t + 1],
+                )
             nc.vector.tensor_tensor(
                 out=y[:, t, :], in0=e[:].indirect(pos2_t[:, lo // 16 : hi // 16]), in1=weight[:, 0:width], op=ALU.mult
             )
             nc.sync.dma_start(out=out_rows[g, :, t, lo:hi], in_=y[:, t, :])
 
-        def round_y(y, g, lo, hi):
+        def round_y(y, g, lo, hi, copy, pieces):
             rounded = keep(f"y_rounded{g}_{lo}", [P, hi - lo, PACK], BF16)
-            nc.vector.tensor_copy(
-                out=rounded[:].rearrange("p (c i) t -> p c t i", i=4), in_=y[:].rearrange("p t (c i) -> p c t i", i=4)
-            )
+            runs = (hi - lo) // 4
+            for piece in range(pieces):
+                cs = slice(piece * runs // pieces, (piece + 1) * runs // pieces)
+                copy(
+                    out=rounded[:].rearrange("p (c i) t -> p c t i", i=4)[:, cs],
+                    in_=y[:].rearrange("p t (c i) -> p c t i", i=4)[:, cs],
+                )
             return rounded
 
         def planes(rounded, g, lo, hi):
@@ -294,26 +325,25 @@ def tile_list_beam_hop_scores_kernel(
         y_first = keep("y_first", [P, PACK, PICKS], F32)
         y_low = keep("y_low", [P, PACK, PICKS // 2], F32)
         y_high = keep("y_high", [P, PACK, PICKS // 2], F32)
+        later = [(0, PACK - 1)] + [(1, t) for t in range(PACK)]
         for t in range(PACK):
             look(e_tiles[0][t], y_first, 0, t, 0, PICKS)
-            if t == 0:
-                scores(0, PACK - 1, 1, nc.scalar.copy)
-            else:
-                scores(1, t - 1, 1, nc.scalar.copy)
-        scores(1, PACK - 1, 1, nc.scalar.copy)
+            scores(later[t][0], later[t][1], 1, nc.scalar.copy)
         e_last = e_tiles[1]
         for t in range(PACK):
             look(e_last[t], y_low, 1, t, 0, PICKS // 2)
             if t == 0:
-                first_rounded = round_y(y_first, 0, 0, PICKS)
+                scores(1, PACK - 1, 1, nc.scalar.copy)
+                first_rounded = round_y(y_first, 0, 0, PICKS, nc.vector.tensor_copy, 1)
             if t == 1:
                 planes(first_rounded, 0, 0, PICKS)
-        low_rounded = round_y(y_low, 1, 0, PICKS // 2)
         for t in range(PACK):
             look(e_last[t], y_high, 1, t, PICKS // 2, PICKS)
             if t == 0:
+                low_rounded = round_y(y_low, 1, 0, PICKS // 2, nc.vector.tensor_copy, 1)
+            if t == 1:
                 planes(low_rounded, 1, 0, PICKS // 2)
-        planes(round_y(y_high, 1, PICKS // 2, PICKS), 1, PICKS // 2, PICKS)
+        planes(round_y(y_high, 1, PICKS // 2, PICKS, nc.vector.tensor_copy, 1), 1, PICKS // 2, PICKS)
         for q in range(QUADS):
             queue = nc.sync if q % 2 == 0 else nc.scalar
             queue.dma_start(out=out_2[:, 4 * q : 4 * q + 4, :].bitcast(I32), in_=y_scales[32 * q : 32 * q + 8, :])

@@ -50,6 +50,11 @@ def tile_list_beam_hop_scores_kernel(
         nc.gpsimd.memset(weight_scale_rows[:], 0)
         nc.vector.memset(v_scales_second[:], 0)
 
+        warm_in = keep("warm_in", [P, 1], F32)
+        warm_out = keep("warm_out", [P, 1], F32)
+        nc.vector.memset(warm_in[:], 0.0)
+        nc.scalar.activation(out=warm_out[:], in_=warm_in[:], func=ACT.Sigmoid)
+
         w1_raw = [keep(f"w1_raw{a}", [P, PACK, H], F32) for a in range(PASSES)]
         wa_raw = [keep(f"wa_raw{g}", [P, PACK, K_PASS], F32) for g in range(GROUPS)]
         tab = [keep(f"tab{a}", [P, T], I32) for a in range(PASSES)]

@@ -102,12 +102,12 @@ def tile_list_beam_hop_scores_kernel(
         for q in range(QUADS):
             load_wb_scales(q, nc.sync if q < QUADS - 1 else nc.gpsimd)
         load_tab(1)
+        nc.sync.dma_start(out=gain_t[:], in_=gain.rearrange("(p t) -> p t", t=PACK))
         v_scales = keep("v_scales", [P, S // 4], I32)
         nc.vector.tensor_copy(out=v_scales[:].bitcast(U8), in_=tab_scale_rows[:].bitcast(U8).indirect(offs_t[:]))
         for q in range(QUADS):
             nc.sync.dma_start(out=v_scales_second[32 * q : 32 * q + 4, :], in_=v_scales[32 * q + 16 : 32 * q + 20, :])
         load_w1(0)
-        nc.sync.dma_start(out=gain_t[:], in_=gain.rearrange("(p t) -> p t", t=PACK))
         load_w1(1)
         nc.sync.dma_start(out=b1_t[:], in_=b1.rearrange("(p t) -> p t", t=PACK))
         load_wa(0)
@@ -201,11 +201,11 @@ def tile_list_beam_hop_scores_kernel(
                 )
             return size
 
-        def apply_gain(half, pair, size):
-            nc.vector.tensor_tensor(
-                out=f_rounded[half][:, 2 * pair * BLOCK : 2 * (pair + 1) * BLOCK, :], in0=size[:],
-                in1=gain_t[:].unsqueeze(1).to_broadcast([P, 2 * BLOCK, PACK]), op=ALU.mult,
-            )
+        gain_rows = keep("gain_rows", [P, 2 * BLOCK, PACK], F32)
+        nc.scalar.copy(out=gain_rows[:], in_=gain_t[:].unsqueeze(1).to_broadcast([P, 2 * BLOCK, PACK]))
+
+        def apply_gain(engine, rounded, size):
+            engine.tensor_tensor(out=rounded, in0=size[:], in1=gain_rows[:], op=ALU.mult)
 
         def h_half(half):
             for block in range(blocks):
@@ -223,18 +223,18 @@ def tile_list_beam_hop_scores_kernel(
         open_banks(f_banks, 0, w2_slice)
         sizes = [[deviation(0, pair) for pair in range(2)]]
         w1_first = round_and_deal("w1_rounded0", w1_raw[0], nc.vector.tensor_copy, 1)
-        w1_second = round_and_deal("w1_rounded1", w1_raw[1], nc.scalar.copy, 4)
-        f_rounded = [keep("f_rounded0", [P, HALF, PACK], BF16, tag="w1_raw0"), keep("f_rounded1", [P, HALF, PACK], BF16)]
+        w1_second = round_and_deal("w1_rounded1", w1_raw[1], nc.vector.tensor_copy, 1)
+        f_rounded = [keep("f_rounded0", [P, HALF, PACK], BF16, tag="w1_raw0")]
         open_banks(f_banks, 1, w2_slice)
         sizes.append([deviation(1, pair) for pair in range(2)])
         quantize(w1_codes[:, 0, :], w1_scales[:, 0, :], w1_first[:])
-        apply_gain(0, 0, sizes[0][0])
+        apply_gain(nc.vector, f_rounded[0][:, 0 : 2 * BLOCK, :], sizes[0][0])
         quantize(w1_codes[:, 1, :], w1_scales[:, 1, :], w1_second[:])
         for half in range(2):
             open_banks(h_banks, half, w1_slice)
             for block in range(blocks):
                 first_stage_pass(h_banks[half, block], half, block, w1_slice, 1)
-        apply_gain(0, 1, sizes[0][1])
+        apply_gain(nc.vector, f_rounded[0][:, 2 * BLOCK : HALF, :], sizes[0][1])
         quantize_half(f_codes, f_scales, f_rounded, 0)
 
         wb_codes = keep("wb_codes", [P, N], U32)
@@ -263,15 +263,19 @@ def tile_list_beam_hop_scores_kernel(
             )
             copy(out=e_tiles[g][t][:, tokens], in_=bank[:])
 
+        f_third = keep("f_third", [P, 2 * BLOCK, PACK], BF16, tag="w1_raw0")
+        apply_gain(nc.gpsimd, f_third[:], sizes[1][0])
         h_half(0)
-        apply_gain(1, 0, sizes[1][0])
-        apply_gain(1, 1, sizes[1][1])
         quantize(wa_codes[:, 0, :], wa_scales[:, 0, :], wa_first[:])
         quantize_half(h_codes, h_scales, h_rounded, 0)
-        quantize_half(f_codes, f_scales, f_rounded, 1)
+        f_fourth = keep("f_fourth", [P, 2 * BLOCK, PACK], BF16, tag="h_rounded0")
+        apply_gain(nc.gpsimd, f_fourth[:], sizes[1][1])
         wa_second = round_and_deal("wa_rounded1", wa_raw[1], nc.scalar.copy, 4)
-        quantize(wa_codes[:, 1, :], wa_scales[:, 1, :], wa_second[:])
         h_half(1)
+        quantize(wa_codes[:, 1, :], wa_scales[:, 1, :], wa_second[:])
+        for quarter, rounded in ((2, f_third), (3, f_fourth)):
+            cols = slice(quarter * 2 * BLOCK, (quarter + 1) * 2 * BLOCK)
+            quantize(f_codes[:, cols], f_scales[:, cols], rounded[:].rearrange("p n t -> p (n t)"))
         for g in range(GROUPS):
             for t in range(PACK):
                 scores(g, t, 0, nc.scalar.copy)

@@ -21,9 +21,16 @@ PACK = 4
 K_PASS = P * PACK
 PASSES = K // K_PASS
 GROUPS = N // K_PASS
+QUADS = 4
+PER_COLUMN = 16
 HALF = S // 2
 BLOCK = 128
-QUADS = 4
+BLOCKS = HALF // BLOCK
+QUARTER = 2 * BLOCK
+
+BANKS_ON_VECTOR = 3
+STEPS_ON_VECTOR = 6
+SCALAR_PIECES = 4
 
 
 def tile_list_beam_hop_scores_kernel(
@@ -39,9 +46,9 @@ def tile_list_beam_hop_scores_kernel(
         def keep(name, shape, dtype, tag=None):
             return held.tile(shape, dtype, name=name, tag=tag or name, align_bytes=64)
 
-        offs_t = held.tile([P, S // 16], U16, name="offs_t")
-        pos1_t = held.tile([P, PICKS // 16], U16, name="pos1_t")
-        pos2_t = held.tile([P, PICKS // 16], U16, name="pos2_t")
+        offs_t = held.tile([P, S // PER_COLUMN], U16, name="offs_t")
+        pos1_t = held.tile([P, PICKS // PER_COLUMN], U16, name="pos1_t")
+        pos2_t = held.tile([P, PICKS // PER_COLUMN], U16, name="pos2_t")
 
         tab_scale_rows = keep("tab_scale_rows", [P, T // 4], I32)
         weight_scale_rows = keep("weight_scale_rows", [P, N // 4], I32)
@@ -103,10 +110,13 @@ def tile_list_beam_hop_scores_kernel(
             load_wb_scales(q, nc.sync if q < QUADS - 1 else nc.gpsimd)
         load_tab(1)
         nc.sync.dma_start(out=gain_t[:], in_=gain.rearrange("(p t) -> p t", t=PACK))
+
         v_scales = keep("v_scales", [P, S // 4], I32)
         nc.vector.tensor_copy(out=v_scales[:].bitcast(U8), in_=tab_scale_rows[:].bitcast(U8).indirect(offs_t[:]))
         for q in range(QUADS):
             nc.sync.dma_start(out=v_scales_second[32 * q : 32 * q + 4, :], in_=v_scales[32 * q + 16 : 32 * q + 20, :])
+        v_planes = [v_scales[:].bitcast(U8), v_scales_second[:].bitcast(U8)]
+
         load_w1(0)
         load_w1(1)
         nc.sync.dma_start(out=b1_t[:], in_=b1.rearrange("(p t) -> p t", t=PACK))
@@ -118,25 +128,19 @@ def tile_list_beam_hop_scores_kernel(
         for vec_t, vec in ((limit_t, limit), (base_t, base), (gy_t, gy)):
             nc.sync.dma_start(out=vec_t[:], in_=vec.rearrange("(g p t) -> p g t", g=GROUPS, t=PACK))
 
-        def round_and_deal(name, raw, copy, pieces):
-            rounded = keep(name, [P, PACK * K_PASS], BF16)
-            for piece in range(pieces):
-                ms = slice(piece * P // pieces, (piece + 1) * P // pieces)
-                copy(
-                    out=rounded[:].rearrange("p (t m j) -> p m j t", t=PACK, j=PACK)[:, ms],
-                    in_=raw[:].rearrange("p j (m t) -> p m j t", t=PACK)[:, ms],
-                )
-            return rounded
+        def round_and_deal(rounded, raw, copy, m0, m1):
+            copy(
+                out=rounded[:].rearrange("p (t m j) -> p m j t", t=PACK, j=PACK)[:, m0:m1],
+                in_=raw[:].rearrange("p j (m t) -> p m j t", t=PACK)[:, m0:m1],
+            )
 
         def quantize(codes, scales, rounded):
             nc.vector.quantize_mx(out=codes.bitcast(E4M3X4), scales=scales, in_=rounded)
 
-        v_planes = [v_scales[:].bitcast(U8), v_scales_second[:].bitcast(U8)]
-
         weight_scales = keep("weight_scales", [P, N], U8)
         nc.vector.tensor_copy(
-            out=weight_scales[:].rearrange("p (a t m) -> p a m t", a=2, t=PACK),
-            in_=weight_scale_rows[:].bitcast(U8).rearrange("p (a m t) -> p a m t", a=2, t=PACK),
+            out=weight_scales[:].rearrange("p (run t m) -> p run m t", run=2, t=PACK),
+            in_=weight_scale_rows[:].bitcast(U8).rearrange("p (run m t) -> p run m t", run=2, t=PACK),
         )
         w2_codes = keep("w2_codes", [P, PASSES * H], U16)
         nc.scalar.copy(
@@ -148,43 +152,37 @@ def tile_list_beam_hop_scores_kernel(
             [keep("v_codes0_0", [P, HALF], U32), keep("v_codes0_1", [P, HALF], U32, tag="weight_scale_rows")],
             [keep("v_codes1_0", [P, HALF], U32), keep("v_codes1_1", [P, HALF], U32)],
         ]
-
-        def gather_words(a, half):
-            cols = slice(half * HALF // 16, (half + 1) * HALF // 16)
-            nc.vector.tensor_copy(out=v_codes[a][half][:], in_=tab[a][:].bitcast(U32).indirect(offs_t[:, cols]))
-
         w1_codes = keep("w1_codes", [P, PASSES, H], U32)
         w1_scales = keep("w1_scales", [P, PASSES, H], U8)
-        gather_words(0, 0)
-        gather_words(0, 1)
-        gather_words(1, 0)
-        gather_words(1, 1)
+        for a in range(PASSES):
+            for half in range(2):
+                entries = offs_t[:, half * HALF // PER_COLUMN : (half + 1) * HALF // PER_COLUMN]
+                nc.vector.tensor_copy(out=v_codes[a][half][:], in_=tab[a][:].bitcast(U32).indirect(entries))
 
         def first_stage_pass(bank, half, block, lhs, a):
-            cols = slice(block * BLOCK, (block + 1) * BLOCK)
-            plane_cols = slice(half * HALF + block * BLOCK, half * HALF + (block + 1) * BLOCK)
+            cells = slice(block * BLOCK, (block + 1) * BLOCK)
+            plane_cells = slice(half * HALF + block * BLOCK, half * HALF + (block + 1) * BLOCK)
             for t in range(PACK):
                 codes, scales = lhs(a, t)
                 nc.tensor.matmul_mx(
                     out=bank[:, t, :], lhsT=codes, lhsT_scale=scales,
-                    rhs=v_codes[a][half][:, cols].bitcast(E4M3X4), rhs_scale=v_planes[a][:, plane_cols],
+                    rhs=v_codes[a][half][:, cells].bitcast(E4M3X4), rhs_scale=v_planes[a][:, plane_cells],
                     start=(a == 0 and t == 0), stop=(a == PASSES - 1 and t == PACK - 1),
                 )
 
         def open_banks(banks, half, lhs):
-            for block in range(HALF // BLOCK):
+            for block in range(BLOCKS):
                 banks[half, block] = psum.tile([P, PACK, BLOCK], F32, name="bank")
                 first_stage_pass(banks[half, block], half, block, lhs, 0)
 
         def w2_slice(a, t):
-            cols = slice(a * H + t * P, a * H + (t + 1) * P)
-            return w2_codes[:, cols].bitcast(U8).bitcast(E2M1X4), weight_scales[:, cols]
+            places = slice(a * H + t * P, a * H + (t + 1) * P)
+            return w2_codes[:, places].bitcast(U8).bitcast(E2M1X4), weight_scales[:, places]
 
         def w1_slice(a, t):
-            cols = slice(t * P, (t + 1) * P)
-            return w1_codes[:, a, cols].bitcast(E4M3X4), w1_scales[:, a, cols]
+            places = slice(t * P, (t + 1) * P)
+            return w1_codes[:, a, places].bitcast(E4M3X4), w1_scales[:, a, places]
 
-        blocks = HALF // BLOCK
         f_codes = keep("f_codes", [P, S], U32)
         f_scales = keep("f_scales", [P, S], U8)
         h_codes = keep("h_codes", [P, S], U32)
@@ -192,7 +190,7 @@ def tile_list_beam_hop_scores_kernel(
         h_rounded = [keep(f"h_rounded{half}", [P, HALF, PACK], BF16) for half in range(2)]
 
         def deviation(half, pair):
-            size = keep(f"size{half}_{pair}", [P, 2 * BLOCK, PACK], F32)
+            size = keep(f"size{half}_{pair}", [P, QUARTER, PACK], F32)
             for b in range(2):
                 bank = f_banks[half, 2 * pair + b]
                 first_stage_pass(bank, half, 2 * pair + b, w2_slice, 1)
@@ -201,87 +199,96 @@ def tile_list_beam_hop_scores_kernel(
                 )
             return size
 
-        gain_rows = keep("gain_rows", [P, 2 * BLOCK, PACK], F32)
-        nc.scalar.copy(out=gain_rows[:], in_=gain_t[:].unsqueeze(1).to_broadcast([P, 2 * BLOCK, PACK]))
+        gain_rows = keep("gain_rows", [P, QUARTER, PACK], F32)
+        nc.scalar.copy(out=gain_rows[:], in_=gain_t[:].unsqueeze(1).to_broadcast([P, QUARTER, PACK]))
 
         def apply_gain(engine, rounded, size):
             engine.tensor_tensor(out=rounded, in0=size[:], in1=gain_rows[:], op=ALU.mult)
 
-        def h_half(half):
-            for block in range(blocks):
-                bank = h_banks[half, block]
+        def add_bias(half):
+            for block in range(BLOCKS):
                 nc.vector.tensor_tensor(
-                    out=h_rounded[half][:, block * BLOCK : (block + 1) * BLOCK, :], in0=bank[:].rearrange("p t n -> p n t"),
+                    out=h_rounded[half][:, block * BLOCK : (block + 1) * BLOCK, :],
+                    in0=h_banks[half, block][:].rearrange("p t n -> p n t"),
                     in1=b1_t[:].unsqueeze(1).to_broadcast([P, BLOCK, PACK]), op=ALU.add,
                 )
 
-        def quantize_half(codes, scales, rounded, half):
-            cols = slice(half * HALF, (half + 1) * HALF)
-            quantize(codes[:, cols], scales[:, cols], rounded[half][:].rearrange("p n t -> p (n t)"))
+        def quantize_cells(codes, scales, rounded, first, count):
+            cells = slice(first, first + count)
+            quantize(codes[:, cells], scales[:, cells], rounded[:].rearrange("p n t -> p (n t)"))
 
         f_banks, h_banks = {}, {}
         open_banks(f_banks, 0, w2_slice)
         sizes = [[deviation(0, pair) for pair in range(2)]]
-        w1_first = round_and_deal("w1_rounded0", w1_raw[0], nc.vector.tensor_copy, 1)
-        w1_second = round_and_deal("w1_rounded1", w1_raw[1], nc.vector.tensor_copy, 1)
-        f_rounded = [keep("f_rounded0", [P, HALF, PACK], BF16, tag="w1_raw0")]
+        w1_rounded = [keep(f"w1_rounded{a}", [P, PACK * H], BF16) for a in range(PASSES)]
+        for a in range(PASSES):
+            round_and_deal(w1_rounded[a], w1_raw[a], nc.vector.tensor_copy, 0, P)
+        f_first_half = keep("f_first_half", [P, HALF, PACK], BF16, tag="w1_raw0")
         open_banks(f_banks, 1, w2_slice)
         sizes.append([deviation(1, pair) for pair in range(2)])
-        quantize(w1_codes[:, 0, :], w1_scales[:, 0, :], w1_first[:])
-        apply_gain(nc.vector, f_rounded[0][:, 0 : 2 * BLOCK, :], sizes[0][0])
-        quantize(w1_codes[:, 1, :], w1_scales[:, 1, :], w1_second[:])
+        quantize(w1_codes[:, 0, :], w1_scales[:, 0, :], w1_rounded[0][:])
+        apply_gain(nc.vector, f_first_half[:, 0:QUARTER, :], sizes[0][0])
+        quantize(w1_codes[:, 1, :], w1_scales[:, 1, :], w1_rounded[1][:])
         for half in range(2):
             open_banks(h_banks, half, w1_slice)
-            for block in range(blocks):
+            for block in range(BLOCKS):
                 first_stage_pass(h_banks[half, block], half, block, w1_slice, 1)
-        apply_gain(nc.vector, f_rounded[0][:, 2 * BLOCK : HALF, :], sizes[0][1])
-        quantize_half(f_codes, f_scales, f_rounded, 0)
+        apply_gain(nc.vector, f_first_half[:, QUARTER:HALF, :], sizes[0][1])
+        quantize_cells(f_codes, f_scales, f_first_half, 0, HALF)
 
         wb_codes = keep("wb_codes", [P, N], U32)
         nc.scalar.copy(
             out=wb_codes[:].rearrange("p (g t m) -> p g m t", g=GROUPS, t=PACK),
             in_=wb_raw[:].bitcast(U32).rearrange("p (g m t) -> p g m t", g=GROUPS, t=PACK),
         )
-        wa_first = round_and_deal("wa_rounded0", wa_raw[0], nc.scalar.copy, 4)
+        wa_rounded = [keep(f"wa_rounded{g}", [P, PACK * K_PASS], BF16) for g in range(GROUPS)]
         wa_codes = keep("wa_codes", [P, GROUPS, K_PASS], U32)
         wa_scales = keep("wa_scales", [P, GROUPS, K_PASS], U8)
+
+        def round_wa(g):
+            for piece in range(SCALAR_PIECES):
+                m0 = piece * P // SCALAR_PIECES
+                round_and_deal(wa_rounded[g], wa_raw[g], nc.scalar.copy, m0, m0 + P // SCALAR_PIECES)
 
         e_tiles = [[keep(f"e{g}_{t}", [P, S], F32) for t in range(PACK)] for g in range(GROUPS)]
 
         def scores(g, t, half, copy):
-            cols = slice(t * P, (t + 1) * P)
-            n_cols = slice(g * K_PASS + t * P, g * K_PASS + (t + 1) * P)
+            places = slice(t * P, (t + 1) * P)
+            wb_places = slice(g * K_PASS + t * P, g * K_PASS + (t + 1) * P)
             bank = psum.tile([P, HALF], F32, name="bank")
-            tokens = slice(half * HALF, (half + 1) * HALF)
+            cells = slice(half * HALF, (half + 1) * HALF)
             nc.tensor.matmul_mx(
-                out=bank[:], lhsT=wb_codes[:, n_cols].bitcast(E4M3X4), lhsT_scale=weight_scales[4:P, n_cols],
-                rhs=f_codes[:, tokens].bitcast(E4M3X4), rhs_scale=f_scales[:, tokens], start=True, stop=False,
+                out=bank[:], lhsT=wb_codes[:, wb_places].bitcast(E4M3X4), lhsT_scale=weight_scales[4:P, wb_places],
+                rhs=f_codes[:, cells].bitcast(E4M3X4), rhs_scale=f_scales[:, cells], start=True, stop=False,
             )
             nc.tensor.matmul_mx(
-                out=bank[:], lhsT=wa_codes[:, g, cols].bitcast(E4M3X4), lhsT_scale=wa_scales[:, g, cols],
-                rhs=h_codes[:, tokens].bitcast(E4M3X4), rhs_scale=h_scales[:, tokens], start=False, stop=True,
+                out=bank[:], lhsT=wa_codes[:, g, places].bitcast(E4M3X4), lhsT_scale=wa_scales[:, g, places],
+                rhs=h_codes[:, cells].bitcast(E4M3X4), rhs_scale=h_scales[:, cells], start=False, stop=True,
             )
-            copy(out=e_tiles[g][t][:, tokens], in_=bank[:])
+            copy(out=e_tiles[g][t][:, cells], in_=bank[:])
 
-        f_third = keep("f_third", [P, 2 * BLOCK, PACK], BF16, tag="w1_raw0")
+        round_wa(0)
+        f_third = keep("f_third", [P, QUARTER, PACK], BF16, tag="w1_raw0")
         apply_gain(nc.gpsimd, f_third[:], sizes[1][0])
-        h_half(0)
-        quantize(wa_codes[:, 0, :], wa_scales[:, 0, :], wa_first[:])
-        quantize_half(h_codes, h_scales, h_rounded, 0)
-        f_fourth = keep("f_fourth", [P, 2 * BLOCK, PACK], BF16, tag="h_rounded0")
+        add_bias(0)
+        quantize(wa_codes[:, 0, :], wa_scales[:, 0, :], wa_rounded[0][:])
+        quantize_cells(h_codes, h_scales, h_rounded[0], 0, HALF)
+        f_fourth = keep("f_fourth", [P, QUARTER, PACK], BF16, tag="h_rounded0")
         apply_gain(nc.gpsimd, f_fourth[:], sizes[1][1])
-        wa_second = round_and_deal("wa_rounded1", wa_raw[1], nc.scalar.copy, 4)
-        h_half(1)
-        quantize(wa_codes[:, 1, :], wa_scales[:, 1, :], wa_second[:])
-        for quarter, rounded in ((2, f_third), (3, f_fourth)):
-            cols = slice(quarter * 2 * BLOCK, (quarter + 1) * 2 * BLOCK)
-            quantize(f_codes[:, cols], f_scales[:, cols], rounded[:].rearrange("p n t -> p (n t)"))
-        for g in range(GROUPS):
-            for t in range(PACK):
-                scores(g, t, 0, nc.scalar.copy)
-        quantize_half(h_codes, h_scales, h_rounded, 1)
-        for t in range(3):
-            scores(0, t, 1, nc.vector.tensor_copy)
+        round_wa(1)
+        add_bias(1)
+        quantize(wa_codes[:, 1, :], wa_scales[:, 1, :], wa_rounded[1][:])
+        quantize_cells(f_codes, f_scales, f_third, HALF, QUARTER)
+        quantize_cells(f_codes, f_scales, f_fourth, HALF + QUARTER, QUARTER)
+
+        tiles_in_order = [(g, t) for g in range(GROUPS) for t in range(PACK)]
+        for g, t in tiles_in_order:
+            scores(g, t, 0, nc.scalar.copy)
+        quantize_cells(h_codes, h_scales, h_rounded[1], HALF, HALF)
+        for g, t in tiles_in_order[:BANKS_ON_VECTOR]:
+            scores(g, t, 1, nc.vector.tensor_copy)
+        second_halves_left = tiles_in_order[BANKS_ON_VECTOR:]
+
         offset_t = keep("offset_t", [P, PACK], F32)
         nc.vector.scalar_tensor_tensor(
             out=offset_t[:], in0=base_t[:, 1, :], scalar=-1.0, in1=gy_t[:, 1, :], op0=ALU.mult, op1=ALU.mult
@@ -291,68 +298,67 @@ def tile_list_beam_hop_scores_kernel(
         y_scales = keep("y_scales", [P, PICKS // 4], I32)
         out_rows = out_0.rearrange("(g p t) m -> g p t m", g=GROUPS, t=PACK)
 
-        def look(e, y, g, t, lo, hi):
-            a_val = ring.tile([P, PICKS], F32, name="a_val")
-            weight = ring.tile([P, PICKS], F32, name="weight")
-            width = hi - lo
+        pieces = [(0, 0, PICKS), (1, 0, PICKS // 2), (1, PICKS // 2, PICKS)]
+        steps = [(g, t, lo, hi) for g, lo, hi in pieces for t in range(PACK)]
+        y_tiles = [keep(f"y{g}_{lo}", [P, PACK, hi - lo], F32) for g, lo, hi in pieces]
+
+        def step(number):
+            g, t, lo, hi = steps[number]
+            y = y_tiles[number // PACK][:, t, :]
+            entries = slice(lo // PER_COLUMN, hi // PER_COLUMN)
+            if number == len(steps) - 1:
+                looked = keep("last_looked", [P, hi - lo], F32)
+            else:
+                looked = ring.tile([P, hi - lo], F32, name="looked")
+            if number < 2:
+                factor = keep(f"first_factor{number}", [P, hi - lo], F32, tag="first_factors")
+            else:
+                factor = ring.tile([P, hi - lo], F32, name="factor")
             nc.scalar.activation(
-                out=a_val[:, 0:width], in_=e[:].indirect(pos1_t[:, lo // 16 : hi // 16]), func=ACT.Sigmoid,
+                out=looked[:], in_=e_tiles[g][t][:].indirect(pos1_t[:, entries]), func=ACT.Sigmoid,
                 bias=limit_t[:, g, t : t + 1],
             )
-            if g == 0:
+            if number < STEPS_ON_VECTOR:
                 nc.vector.tensor_scalar(
-                    out=weight[:, 0:width], in0=a_val[:, 0:width], scalar1=base_t[:, g, t : t + 1],
-                    scalar2=gy_t[:, g, t : t + 1], op0=ALU.subtract, op1=ALU.mult,
+                    out=factor[:], in0=looked[:], scalar1=base_t[:, g, t : t + 1], scalar2=gy_t[:, g, t : t + 1],
+                    op0=ALU.subtract, op1=ALU.mult,
                 )
             else:
                 nc.scalar.activation(
-                    out=weight[:, 0:width], in_=a_val[:, 0:width], func=ACT.Identity,
+                    out=factor[:], in_=looked[:], func=ACT.Identity,
                     scale=gy_t[:, g, t : t + 1], bias=offset_t[:, t : t + 1],
                 )
-            nc.vector.tensor_tensor(
-                out=y[:, t, :], in0=e[:].indirect(pos2_t[:, lo // 16 : hi // 16]), in1=weight[:, 0:width], op=ALU.mult
-            )
-            nc.sync.dma_start(out=out_rows[g, :, t, lo:hi], in_=y[:, t, :])
+            nc.vector.tensor_tensor(out=y, in0=e_tiles[g][t][:].indirect(pos2_t[:, entries]), in1=factor[:], op=ALU.mult)
+            nc.sync.dma_start(out=out_rows[g, :, t, lo:hi], in_=y)
 
-        def round_y(y, g, lo, hi, copy, pieces):
-            rounded = keep(f"y_rounded{g}_{lo}", [P, hi - lo, PACK], BF16)
-            runs = (hi - lo) // 4
-            for piece in range(pieces):
-                cs = slice(piece * runs // pieces, (piece + 1) * runs // pieces)
-                copy(
-                    out=rounded[:].rearrange("p (c i) t -> p c t i", i=4)[:, cs],
-                    in_=y[:].rearrange("p t (c i) -> p c t i", i=4)[:, cs],
-                )
-            return rounded
+        def round_y(rounded, y, copy):
+            copy(out=rounded.rearrange("p (c i) t -> p c t i", i=4), in_=y[:].rearrange("p t (c i) -> p c t i", i=4))
 
         def planes(rounded, g, lo, hi):
-            quantize(y_codes[:, g, lo:hi], y_scales[4 * g : P, :].bitcast(U8)[:, lo:hi], rounded[:].rearrange("p m t -> p (m t)"))
+            quantize(
+                y_codes[:, g, lo:hi], y_scales[4 * g : P, :].bitcast(U8)[:, lo:hi], rounded[:].rearrange("p m t -> p (m t)")
+            )
             nc.sync.dma_start(
                 out=out_1[g].rearrange("p m i -> p (m i)").bitcast(I32)[:, lo:hi], in_=y_codes[:, g, lo:hi]
             )
 
-        y_first = keep("y_first", [P, PACK, PICKS], F32)
-        y_low = keep("y_low", [P, PACK, PICKS // 2], F32)
-        y_high = keep("y_high", [P, PACK, PICKS // 2], F32)
-        later = [(0, PACK - 1)] + [(1, t) for t in range(PACK)]
-        for t in range(PACK):
-            look(e_tiles[0][t], y_first, 0, t, 0, PICKS)
-            scores(later[t][0], later[t][1], 1, nc.scalar.copy)
-        e_last = e_tiles[1]
-        for t in range(PACK):
-            look(e_last[t], y_low, 1, t, 0, PICKS // 2)
-            if t == 0:
-                scores(1, PACK - 1, 1, nc.scalar.copy)
-                first_rounded = round_y(y_first, 0, 0, PICKS, nc.vector.tensor_copy, 1)
-            if t == 1:
+        first_rounded = keep("first_rounded", [P, PICKS, PACK], BF16)
+        for number in range(len(steps)):
+            step(number)
+            if number < len(second_halves_left):
+                g, t = second_halves_left[number]
+                scores(g, t, 1, nc.scalar.copy)
+            if number == PACK:
+                round_y(first_rounded[:], y_tiles[0], nc.vector.tensor_copy)
+            if number == PACK + 1:
                 planes(first_rounded, 0, 0, PICKS)
-        for t in range(PACK):
-            look(e_last[t], y_high, 1, t, PICKS // 2, PICKS)
-            if t == 0:
-                low_rounded = round_y(y_low, 1, 0, PICKS // 2, nc.vector.tensor_copy, 1)
-            if t == 1:
-                planes(low_rounded, 1, 0, PICKS // 2)
-        planes(round_y(y_high, 1, PICKS // 2, PICKS, nc.vector.tensor_copy, 1), 1, PICKS // 2, PICKS)
+
+        lower_rounded = keep("lower_rounded", [P, PICKS // 2, PACK], BF16, tag="last_looked")
+        upper_rounded = keep("upper_rounded", [P, PICKS // 2, PACK], BF16)
+        round_y(lower_rounded[:], y_tiles[1], nc.scalar.copy)
+        round_y(upper_rounded[:], y_tiles[2], nc.vector.tensor_copy)
+        planes(lower_rounded, 1, 0, PICKS // 2)
+        planes(upper_rounded, 1, PICKS // 2, PICKS)
         for q in range(QUADS):
             queue = nc.sync if q % 2 == 0 else nc.scalar
             queue.dma_start(out=out_2[:, 4 * q : 4 * q + 4, :].bitcast(I32), in_=y_scales[32 * q : 32 * q + 8, :])

from contextlib import ExitStack

import concourse.mybir as mybir

K, T, S, PICKS, H, N = 1024, 2048, 1024, 512, 512, 1024
FLOPS = 2 * (2 * K * H * S + 2 * H * N * S)

F32 = mybir.dt.float32
BF16 = mybir.dt.bfloat16
I32 = mybir.dt.int32
U32 = mybir.dt.uint32
U16 = mybir.dt.uint16
U8 = mybir.dt.uint8
E4M3X4 = mybir.dt.float8_e4m3fn_x4
E2M1X4 = mybir.dt.float4_e2m1fn_x4
ALU = mybir.AluOpType
ACT = mybir.ActivationFunctionType

P = 128
PACK = 4
K_PASS = P * PACK
PASSES = K // K_PASS
GROUPS = N // K_PASS
QUADS = 4
PER_COLUMN = 16
HALF = S // 2
BLOCK = 128
BLOCKS = HALF // BLOCK
QUARTER = 2 * BLOCK

BANKS_ON_VECTOR = 3
STEPS_ON_VECTOR = 6
SCALAR_PIECES = 4


def tile_list_beam_hop_scores_kernel(
    tc, tab_words, tab_scales, offs, pos1, pos2, w1, b1, w2_words, w2_scales, gain, wa, wb_words, wb_scales,
    limit, base, gy, out_0, out_1, out_2,
):
    nc = tc.nc
    with ExitStack() as ctx:
        held = ctx.enter_context(tc.tile_pool(name="held", bufs=1))
        ring = ctx.enter_context(tc.tile_pool(name="ring", bufs=3))
        psum = ctx.enter_context(tc.psum_pool(name="psum", bufs=8))

        def keep(name, shape, dtype, tag=None):
            return held.tile(shape, dtype, name=name, tag=tag or name, align_bytes=64)

        offs_t = held.tile([P, S // PER_COLUMN], U16, name="offs_t")
        pos1_t = held.tile([P, PICKS // PER_COLUMN], U16, name="pos1_t")
        pos2_t = held.tile([P, PICKS // PER_COLUMN], U16, name="pos2_t")

        tab_scale_rows = keep("tab_scale_rows", [P, T // 4], I32)
        weight_scale_rows = keep("weight_scale_rows", [P, N // 4], I32)
        v_scales_second = keep("v_scales_second", [P, S // 4], I32)
        nc.vector.memset(tab_scale_rows[:], 0)
        nc.gpsimd.memset(weight_scale_rows[:], 0)
        nc.vector.memset(v_scales_second[:], 0)

        warm_in = keep("warm_in", [P, 1], F32)
        warm_out = keep("warm_out", [P, 1], F32)
        nc.vector.memset(warm_in[:], 0.0)
        nc.scalar.activation(out=warm_out[:], in_=warm_in[:], func=ACT.Sigmoid)

        w1_raw = [keep(f"w1_raw{a}", [P, PACK, H], F32) for a in range(PASSES)]
        wa_raw = [keep(f"wa_raw{g}", [P, PACK, K_PASS], F32) for g in range(GROUPS)]
        tab = [keep(f"tab{a}", [P, T], I32) for a in range(PASSES)]
        w2_raw = keep("w2_raw", [P, PASSES, H // 2], I32)
        wb_raw = keep("wb_raw", [P, N], I32)
        b1_t = keep("b1_t", [P, PACK], F32)
        gain_t = keep("gain_t", [P, PACK], F32)
        limit_t = keep("limit_t", [P, GROUPS, PACK], F32)
        base_t = keep("base_t", [P, GROUPS, PACK], F32)
        gy_t = keep("gy_t", [P, GROUPS, PACK], F32)

        def load_w1(a):
            nc.sync.dma_start(out=w1_raw[a][:], in_=w1[a * K_PASS : (a + 1) * K_PASS, :].rearrange("(p j) c -> p j c", j=PACK))

        def load_tab(a):
            nc.sync.dma_start(out=tab[a][:], in_=tab_words[a].rearrange("p t i -> p (t i)").bitcast(I32))

        def load_wa(g):
            nc.sync.dma_start(
                out=wa_raw[g][:], in_=wa[:, g * K_PASS : (g + 1) * K_PASS].rearrange("(p j) c -> p j c", j=PACK)
            )

        def load_w2_scales(q):
            nc.sync.dma_start(
                out=weight_scale_rows[32 * q : 32 * q + 4, :].rearrange("r (a c) -> r a c", a=PASSES),
                in_=w2_scales[:, 4 * q : 4 * q + 4, :].bitcast(I32).rearrange("a r c -> r a c"),
            )

        def load_wb_scales(q, queue):
            queue.dma_start(
                out=weight_scale_rows[32 * q + 4 : 32 * q + 8, :], in_=wb_scales[0, 4 * q : 4 * q + 4, :].bitcast(I32)
            )

        nc.sync.dma_start(offs_t[:], offs)
        for r in range(4):
            nc.sync.dma_start(
                out=tab_scale_rows[r:P:16, :],
                in_=tab_scales.bitcast(I32).rearrange("a (q r) c -> r q a c", r=4)[r],
            )
        nc.sync.dma_start(out=w2_raw[:], in_=w2_words.bitcast(I32).rearrange("a p c -> p a c"))
        load_w2_scales(0)
        load_tab(0)
        for q in range(1, QUADS):
            load_w2_scales(q)
        for q in range(QUADS):
            load_wb_scales(q, nc.sync if q < QUADS - 1 else nc.gpsimd)
        load_tab(1)
        nc.sync.dma_start(out=gain_t[:], in_=gain.rearrange("(p t) -> p t", t=PACK))

        v_scales = keep("v_scales", [P, S // 4], I32)
        nc.vector.tensor_copy(out=v_scales[:].bitcast(U8), in_=tab_scale_rows[:].bitcast(U8).indirect(offs_t[:]))
        for q in range(QUADS):
            nc.sync.dma_start(out=v_scales_second[32 * q : 32 * q + 4, :], in_=v_scales[32 * q + 16 : 32 * q + 20, :])
        v_planes = [v_scales[:].bitcast(U8), v_scales_second[:].bitcast(U8)]

        load_w1(0)
        load_w1(1)
        nc.sync.dma_start(out=b1_t[:], in_=b1.rearrange("(p t) -> p t", t=PACK))
        load_wa(0)
        nc.sync.dma_start(out=wb_raw[:], in_=wb_words[0].rearrange("p c i -> p (c i)").bitcast(I32))
        nc.sync.dma_start(pos1_t[:], pos1)
        nc.sync.dma_start(pos2_t[:], pos2)
        load_wa(1)
        for vec_t, vec in ((limit_t, limit), (base_t, base), (gy_t, gy)):
            nc.sync.dma_start(out=vec_t[:], in_=vec.rearrange("(g p t) -> p g t", g=GROUPS, t=PACK))

        def round_and_deal(rounded, raw, copy, m0, m1):
            copy(
                out=rounded[:].rearrange("p (t m j) -> p m j t", t=PACK, j=PACK)[:, m0:m1],
                in_=raw[:].rearrange("p j (m t) -> p m j t", t=PACK)[:, m0:m1],
            )

        def quantize(codes, scales, rounded):
            nc.vector.quantize_mx(out=codes.bitcast(E4M3X4), scales=scales, in_=rounded)

        weight_scales = keep("weight_scales", [P, N], U8)
        nc.vector.tensor_copy(
            out=weight_scales[:].rearrange("p (run t m) -> p run m t", run=2, t=PACK),
            in_=weight_scale_rows[:].bitcast(U8).rearrange("p (run m t) -> p run m t", run=2, t=PACK),
        )
        w2_codes = keep("w2_codes", [P, PASSES * H], U16)
        nc.scalar.copy(
            out=w2_codes[:].rearrange("p (a t m) -> p a m t", a=PASSES, t=PACK),
            in_=w2_raw[:].rearrange("p a c -> p (a c)").bitcast(U16).rearrange("p (a m t) -> p a m t", a=PASSES, t=PACK),
        )

        v_codes = [
            [keep("v_codes0_0", [P, HALF], U32), keep("v_codes0_1", [P, HALF], U32, tag="weight_scale_rows")],
            [keep("v_codes1_0", [P, HALF], U32), keep("v_codes1_1", [P, HALF], U32)],
        ]
        w1_codes = keep("w1_codes", [P, PASSES, H], U32)
        w1_scales = keep("w1_scales", [P, PASSES, H], U8)
        for a in range(PASSES):
            for half in range(2):
                entries = offs_t[:, half * HALF // PER_COLUMN : (half + 1) * HALF // PER_COLUMN]
                nc.vector.tensor_copy(out=v_codes[a][half][:], in_=tab[a][:].bitcast(U32).indirect(entries))

        def first_stage_pass(bank, half, block, lhs, a):
            cells = slice(block * BLOCK, (block + 1) * BLOCK)
            plane_cells = slice(half * HALF + block * BLOCK, half * HALF + (block + 1) * BLOCK)
            for t in range(PACK):
                codes, scales = lhs(a, t)
                nc.tensor.matmul_mx(
                    out=bank[:, t, :], lhsT=codes, lhsT_scale=scales,
                    rhs=v_codes[a][half][:, cells].bitcast(E4M3X4), rhs_scale=v_planes[a][:, plane_cells],
                    start=(a == 0 and t == 0), stop=(a == PASSES - 1 and t == PACK - 1),
                )

        def open_banks(banks, half, lhs):
            for block in range(BLOCKS):
                banks[half, block] = psum.tile([P, PACK, BLOCK], F32, name="bank")
                first_stage_pass(banks[half, block], half, block, lhs, 0)

        def w2_slice(a, t):
            places = slice(a * H + t * P, a * H + (t + 1) * P)
            return w2_codes[:, places].bitcast(U8).bitcast(E2M1X4), weight_scales[:, places]

        def w1_slice(a, t):
            places = slice(t * P, (t + 1) * P)
            return w1_codes[:, a, places].bitcast(E4M3X4), w1_scales[:, a, places]

        f_codes = keep("f_codes", [P, S], U32)
        f_scales = keep("f_scales", [P, S], U8)
        h_codes = keep("h_codes", [P, S], U32)
        h_scales = keep("h_scales", [P, S], U8)
        h_rounded = [keep(f"h_rounded{half}", [P, HALF, PACK], BF16) for half in range(2)]

        def deviation(half, pair):
            size = keep(f"size{half}_{pair}", [P, QUARTER, PACK], F32)
            for b in range(2):
                bank = f_banks[half, 2 * pair + b]
                first_stage_pass(bank, half, 2 * pair + b, w2_slice, 1)
                nc.scalar.activation(
                    out=size[:, b * BLOCK : (b + 1) * BLOCK, :], in_=bank[:].rearrange("p t n -> p n t"), func=ACT.Abs
                )
            return size

        gain_rows = keep("gain_rows", [P, QUARTER, PACK], F32)
        nc.scalar.copy(out=gain_rows[:], in_=gain_t[:].unsqueeze(1).to_broadcast([P, QUARTER, PACK]))

        def apply_gain(engine, rounded, size):
            engine.tensor_tensor(out=rounded, in0=size[:], in1=gain_rows[:], op=ALU.mult)

        def add_bias(half):
            for block in range(BLOCKS):
                nc.vector.tensor_tensor(
                    out=h_rounded[half][:, block * BLOCK : (block + 1) * BLOCK, :],
                    in0=h_banks[half, block][:].rearrange("p t n -> p n t"),
                    in1=b1_t[:].unsqueeze(1).to_broadcast([P, BLOCK, PACK]), op=ALU.add,
                )

        def quantize_cells(codes, scales, rounded, first, count):
            cells = slice(first, first + count)
            quantize(codes[:, cells], scales[:, cells], rounded[:].rearrange("p n t -> p (n t)"))

        f_banks, h_banks = {}, {}
        open_banks(f_banks, 0, w2_slice)
        sizes = [[deviation(0, pair) for pair in range(2)]]
        w1_rounded = [keep(f"w1_rounded{a}", [P, PACK * H], BF16) for a in range(PASSES)]
        for a in range(PASSES):
            round_and_deal(w1_rounded[a], w1_raw[a], nc.vector.tensor_copy, 0, P)
        f_first_half = keep("f_first_half", [P, HALF, PACK], BF16, tag="w1_raw0")
        open_banks(f_banks, 1, w2_slice)
        sizes.append([deviation(1, pair) for pair in range(2)])
        quantize(w1_codes[:, 0, :], w1_scales[:, 0, :], w1_rounded[0][:])
        apply_gain(nc.vector, f_first_half[:, 0:QUARTER, :], sizes[0][0])
        quantize(w1_codes[:, 1, :], w1_scales[:, 1, :], w1_rounded[1][:])
        for half in range(2):
            open_banks(h_banks, half, w1_slice)
            for block in range(BLOCKS):
                first_stage_pass(h_banks[half, block], half, block, w1_slice, 1)
        apply_gain(nc.vector, f_first_half[:, QUARTER:HALF, :], sizes[0][1])
        quantize_cells(f_codes, f_scales, f_first_half, 0, HALF)

        wb_codes = keep("wb_codes", [P, N], U32)
        nc.scalar.copy(
            out=wb_codes[:].rearrange("p (g t m) -> p g m t", g=GROUPS, t=PACK),
            in_=wb_raw[:].bitcast(U32).rearrange("p (g m t) -> p g m t", g=GROUPS, t=PACK),
        )
        wa_rounded = [keep(f"wa_rounded{g}", [P, PACK * K_PASS], BF16) for g in range(GROUPS)]
        wa_codes = keep("wa_codes", [P, GROUPS, K_PASS], U32)
        wa_scales = keep("wa_scales", [P, GROUPS, K_PASS], U8)

        def round_wa(g):
            for piece in range(SCALAR_PIECES):
                m0 = piece * P // SCALAR_PIECES
                round_and_deal(wa_rounded[g], wa_raw[g], nc.scalar.copy, m0, m0 + P // SCALAR_PIECES)

        e_tiles = [[keep(f"e{g}_{t}", [P, S], F32) for t in range(PACK)] for g in range(GROUPS)]

        def scores(g, t, half, copy):
            places = slice(t * P, (t + 1) * P)
            wb_places = slice(g * K_PASS + t * P, g * K_PASS + (t + 1) * P)
            bank = psum.tile([P, HALF], F32, name="bank")
            cells = slice(half * HALF, (half + 1) * HALF)
            nc.tensor.matmul_mx(
                out=bank[:], lhsT=wb_codes[:, wb_places].bitcast(E4M3X4), lhsT_scale=weight_scales[4:P, wb_places],
                rhs=f_codes[:, cells].bitcast(E4M3X4), rhs_scale=f_scales[:, cells], start=True, stop=False,
            )
            nc.tensor.matmul_mx(
                out=bank[:], lhsT=wa_codes[:, g, places].bitcast(E4M3X4), lhsT_scale=wa_scales[:, g, places],
                rhs=h_codes[:, cells].bitcast(E4M3X4), rhs_scale=h_scales[:, cells], start=False, stop=True,
            )
            copy(out=e_tiles[g][t][:, cells], in_=bank[:])

        round_wa(0)
        f_third = keep("f_third", [P, QUARTER, PACK], BF16, tag="w1_raw0")
        apply_gain(nc.gpsimd, f_third[:], sizes[1][0])
        add_bias(0)
        quantize(wa_codes[:, 0, :], wa_scales[:, 0, :], wa_rounded[0][:])
        quantize_cells(h_codes, h_scales, h_rounded[0], 0, HALF)
        f_fourth = keep("f_fourth", [P, QUARTER, PACK], BF16, tag="h_rounded0")
        apply_gain(nc.gpsimd, f_fourth[:], sizes[1][1])
        round_wa(1)
        add_bias(1)
        quantize(wa_codes[:, 1, :], wa_scales[:, 1, :], wa_rounded[1][:])
        quantize_cells(f_codes, f_scales, f_third, HALF, QUARTER)
        quantize_cells(f_codes, f_scales, f_fourth, HALF + QUARTER, QUARTER)

        tiles_in_order = [(g, t) for g in range(GROUPS) for t in range(PACK)]
        for g, t in tiles_in_order:
            scores(g, t, 0, nc.scalar.copy)
        quantize_cells(h_codes, h_scales, h_rounded[1], HALF, HALF)
        for g, t in tiles_in_order[:BANKS_ON_VECTOR]:
            scores(g, t, 1, nc.vector.tensor_copy)
        second_halves_left = tiles_in_order[BANKS_ON_VECTOR:]

        offset_t = keep("offset_t", [P, PACK], F32)
        nc.vector.scalar_tensor_tensor(
            out=offset_t[:], in0=base_t[:, 1, :], scalar=-1.0, in1=gy_t[:, 1, :], op0=ALU.mult, op1=ALU.mult
        )

        y_codes = keep("y_codes", [P, GROUPS, PICKS], I32)
        y_scales = keep("y_scales", [P, PICKS // 4], I32)
        out_rows = out_0.rearrange("(g p t) m -> g p t m", g=GROUPS, t=PACK)

        pieces = [(0, 0, PICKS), (1, 0, PICKS // 2), (1, PICKS // 2, PICKS)]
        steps = [(g, t, lo, hi) for g, lo, hi in pieces for t in range(PACK)]
        y_tiles = [keep(f"y{g}_{lo}", [P, PACK, hi - lo], F32) for g, lo, hi in pieces]

        def step(number):
            g, t, lo, hi = steps[number]
            y = y_tiles[number // PACK][:, t, :]
            entries = slice(lo // PER_COLUMN, hi // PER_COLUMN)
            if number == len(steps) - 1:
                looked = keep("last_looked", [P, hi - lo], F32)
            else:
                looked = ring.tile([P, hi - lo], F32, name="looked")
            if number < 2:
                factor = keep(f"first_factor{number}", [P, hi - lo], F32, tag="first_factors")
            else:
                factor = ring.tile([P, hi - lo], F32, name="factor")
            nc.scalar.activation(
                out=looked[:], in_=e_tiles[g][t][:].indirect(pos1_t[:, entries]), func=ACT.Sigmoid,
                bias=limit_t[:, g, t : t + 1],
            )
            if number < STEPS_ON_VECTOR:
                nc.vector.tensor_scalar(
                    out=factor[:], in0=looked[:], scalar1=base_t[:, g, t : t + 1], scalar2=gy_t[:, g, t : t + 1],
                    op0=ALU.subtract, op1=ALU.mult,
                )
            else:
                nc.scalar.activation(
                    out=factor[:], in_=looked[:], func=ACT.Identity,
                    scale=gy_t[:, g, t : t + 1], bias=offset_t[:, t : t + 1],
                )
            nc.vector.tensor_tensor(out=y, in0=e_tiles[g][t][:].indirect(pos2_t[:, entries]), in1=factor[:], op=ALU.mult)
            nc.sync.dma_start(out=out_rows[g, :, t, lo:hi], in_=y)

        def round_y(rounded, y, copy):
            copy(out=rounded.rearrange("p (c i) t -> p c t i", i=4), in_=y[:].rearrange("p t (c i) -> p c t i", i=4))

        def planes(rounded, g, lo, hi):
            quantize(
                y_codes[:, g, lo:hi], y_scales[4 * g : P, :].bitcast(U8)[:, lo:hi], rounded[:].rearrange("p m t -> p (m t)")
            )
            nc.sync.dma_start(
                out=out_1[g].rearrange("p m i -> p (m i)").bitcast(I32)[:, lo:hi], in_=y_codes[:, g, lo:hi]
            )

        first_rounded = keep("first_rounded", [P, PICKS, PACK], BF16)
        for number in range(len(steps)):
            step(number)
            if number < len(second_halves_left):
                g, t = second_halves_left[number]
                scores(g, t, 1, nc.scalar.copy)
            if number == PACK:
                round_y(first_rounded[:], y_tiles[0], nc.vector.tensor_copy)
            if number == PACK + 1:
                planes(first_rounded, 0, 0, PICKS)

        lower_rounded = keep("lower_rounded", [P, PICKS // 2, PACK], BF16, tag="last_looked")
        upper_rounded = keep("upper_rounded", [P, PICKS // 2, PACK], BF16)
        round_y(lower_rounded[:], y_tiles[1], nc.scalar.copy)
        round_y(upper_rounded[:], y_tiles[2], nc.vector.tensor_copy)
        planes(lower_rounded, 1, 0, PICKS // 2)
        planes(upper_rounded, 1, PICKS // 2, PICKS)
        for q in range(QUADS):
            queue = nc.sync if q % 2 == 0 else nc.scalar
            queue.dma_start(out=out_2[:, 4 * q : 4 * q + 4, :].bitcast(I32), in_=y_scales[32 * q : 32 * q + 8, :])
